import numpy as np
import ml_dtypes


def mxq(x, axis, fmt="e4m3"):
    dtype, down = {"e4m3": (ml_dtypes.float8_e4m3fn, 7), "e5m2": (ml_dtypes.float8_e5m2, 14)}[fmt]
    v = np.moveaxis(np.asarray(x, np.float32).astype(ml_dtypes.bfloat16).astype(np.float64), axis, -1)
    blocks = v.reshape(v.shape[:-1] + (-1, 32))
    amax = np.abs(blocks).max(-1, keepdims=True)
    byte = np.maximum(np.where(amax > 0, np.frexp(amax)[1] - 1 + 127, 0) - down, 1)
    scale = np.exp2(byte - 127.0)
    codes = (blocks / scale).astype(np.float32).astype(dtype).astype(np.float64)
    return np.moveaxis((codes * scale).reshape(v.shape), -1, axis)


WIDE = False


def mx_kscale(k):
    if not WIDE:
        return np.ones(k)
    levels = np.array([10, -10, 5, -5, 0])
    if k % 512:
        return np.exp2(np.random.permutation(np.resize(levels, k // 32))).repeat(32)
    a = np.empty((k // 512, 16))
    for p in range(k // 512):
        a[p, :8] = np.random.permutation(np.resize(levels, 8))
        for g in range(8):
            far = levels[np.abs(levels - a[p, g]) >= 10]
            a[p, g + 8] = far[np.random.randint(len(far))]
    return np.exp2(a.ravel()).repeat(32)


def f64(x):
    return np.asarray(x).astype(np.float64)


def striped(idx):
    return np.tile(idx.reshape(-1, 16).T, (8, 1)).astype(np.uint16)


def unstriped(offs):
    return offs[:16].T.reshape(-1).astype(np.int64)


def striped8(idx):
    return np.concatenate([x.reshape(-1, 16).T for x in idx]).astype(np.uint16)


def runs(offs, k):
    lists = np.stack([offs[16 * r : 16 * r + 16].T.reshape(-1) for r in range(8)]).astype(np.int64)
    return lists[np.arange(k) % 512 // 64]


def pack_weight(w):
    k, n = w.shape
    w = f64(np.asarray(w, np.float32).astype(ml_dtypes.bfloat16)).reshape(k // 32, 32, n)
    amax = np.abs(w).max(1)
    byte = np.clip(np.where(amax > 0, np.frexp(amax)[1] - 1 + 127 - 7, 1), 1, 254)
    scaled = (w * np.exp2(127.0 - byte)[:, None, :]).reshape(k, n).astype(np.float32)
    words = np.ascontiguousarray(scaled.reshape(k // 512, 128, 4, n).transpose(0, 1, 3, 2)).astype(ml_dtypes.float8_e4m3fn).view(np.uint8)
    return words, np.ascontiguousarray(byte.astype(np.uint8).reshape(k // 512, 16, n))


def unpack_weight(words, scales):
    g, p, n, _ = words.shape
    vals = np.ascontiguousarray(words).view(ml_dtypes.float8_e4m3fn).astype(np.float64) * np.repeat(np.exp2(scales.astype(np.float64) - 127.0), 8, axis=1)[..., None]
    return vals.transpose(0, 1, 3, 2).reshape(g * 512, n)


E2M1 = np.array([0.0, 0.5, 1.0, 1.5, 2.0, 3.0, 4.0, 6.0, -0.0, -0.5, -1.0, -1.5, -2.0, -3.0, -4.0, -6.0])


def pack_fp4(w):
    k, n = w.shape
    w = f64(np.asarray(w, np.float32).astype(ml_dtypes.bfloat16)).reshape(k // 32, 32, n)
    amax = np.abs(w).max(1)
    mant, ex = np.frexp(amax / 6.0)
    byte = np.clip(np.where(amax > 0, np.where(mant > 0.5, ex, ex - 1) + 127, 1), 1, 254)
    scaled = (w * np.exp2(127.0 - byte)[:, None, :]).reshape(k, n).astype(np.float32)
    c = np.ascontiguousarray(scaled.reshape(k // 512, 128, 4, n).transpose(0, 1, 3, 2)).astype(ml_dtypes.float4_e2m1fn).view(np.uint8) & 0xF
    words = (c[..., 0::2] | (c[..., 1::2] << 4)).reshape(k // 512, 128, 2 * n)
    return np.ascontiguousarray(words), np.ascontiguousarray(byte.astype(np.uint8).reshape(k // 512, 16, n))


def unpack_fp4(words, scales):
    g, _, n = scales.shape
    words = np.ascontiguousarray(words).reshape(g, 128, n, 2)
    nib = np.empty((g, 128, n, 4), np.uint8)
    nib[..., 0::2] = words & 0xF
    nib[..., 1::2] = words >> 4
    vals = E2M1[nib] * np.repeat(np.exp2(scales.astype(np.float64) - 127.0), 8, axis=1)[..., None]
    return vals.transpose(0, 1, 3, 2).reshape(g * 512, n)


K, T, S, N, G, H, W = 512, 2048, 512, 512, 2048, 512, 256


def setup_inputs():
    n = np.random.standard_normal
    s = mx_kscale(K)[:, None]
    u = mx_kscale(S)
    packed_xT = pack_weight(n((K, T)) * s)
    packed_dT = pack_weight(n((K, G)) / s)
    packed_w1 = pack_fp4(n((H, N)) / np.sqrt(H) / u[:, None])
    perm = np.stack([np.random.permutation(S) for _ in range(8)])
    return {
        "x_words": packed_xT[0],
        "x_scales": packed_xT[1],
        "d_words": packed_dT[0],
        "d_scales": packed_dT[1],
        "gn": (np.random.uniform(0.5, 1.5, (H, 1)) * u[:, None]).astype(np.float32),
        "w1_words": packed_w1[0],
        "w1_scales": packed_w1[1],
        "offs": striped8(np.random.randint(0, T, (8, S))),
        "ci": striped(np.random.permutation(G)[:H]),
        "n1": striped8(perm[:, :W]),
        "n2": striped8(perm[:, W:]),
        "n3": striped8(np.stack([np.random.permutation(S) for _ in range(8)])),
        "n4": striped8(np.stack([np.random.permutation(S) for _ in range(8)])),
    }


def reference(x_words, x_scales, d_words, d_scales, gn, w1_words, w1_scales, offs, ci, n1, n2, n3, n4):
    d_ci = unpack_weight(d_words, d_scales)[:, unstriped(ci)]
    xq = unpack_weight(x_words, x_scales)[np.arange(K)[:, None], runs(offs, K)]
    s = 0.0625 * (d_ci.T @ xq)
    pa = s[np.arange(H)[:, None], runs(n1, H)]
    pb = s[np.arange(H)[:, None], runs(n2, H)]
    rb = np.maximum(pa, pb)
    ra = pa / (np.abs(pb) + 0.5)
    ds = np.zeros((H, S))
    ds[np.arange(H)[:, None], runs(n1, H)] = ra
    dt = ds.copy()
    dt[np.arange(H)[:, None], runs(n2, H)] = rb
    z = f64(gn) * dt
    h = unpack_fp4(w1_words, w1_scales).T @ mxq(z, 0, "e4m3")
    st = np.maximum(h, h[np.arange(N)[:, None], runs(n3, N)])
    ds2 = np.zeros((N, S))
    ds2[np.arange(N)[:, None], runs(n4, N)] = st
    return ds2 - h

@@ -1,0 +1,197 @@
+from contextlib import ExitStack
+
+import concourse.mybir as mybir
+
+F32 = mybir.dt.float32
+BF16 = mybir.dt.bfloat16
+I32 = mybir.dt.int32
+U32 = mybir.dt.uint32
+U16 = mybir.dt.uint16
+U8 = mybir.dt.uint8
+FP8X4 = mybir.dt.float8_e4m3fn_x4
+FP4X4 = mybir.dt.float4_e2m1fn_x4
+ALU = mybir.AluOpType
+ACT = mybir.ActivationFunctionType
+
+P = 128
+PACK = 4
+T = 2048
+S = 512
+W = 256
+
+FLOPS = 2 * 2 * 512 * 512 * 512
+
+
+def tile_picked_hwlratiosendhop_none_p_kernel(
+    tc, x_words, x_scales, d_words, d_scales, gn, w1_words, w1_scales, offs, ci, n1, n2, n3, n4, out
+):
+    nc = tc.nc
+    with ExitStack() as ctx:
+        keep = ctx.enter_context(tc.tile_pool(name="keep", bufs=1))
+        psum = ctx.enter_context(tc.psum_pool(name="psum", bufs=1))
+
+        def load_list(name, src):
+            t = keep.tile(list(src.shape), U16, name=name)
+            nc.sync.dma_start(t[:], src)
+            return t
+
+        offs_t = load_list("offs_t", offs)
+        ci_t = load_list("ci_t", ci)
+        xs_tab = keep.tile([P, T], U8, name="xs_tab", align_bytes=64)
+        ds_tab = keep.tile([P, T], U8, name="ds_tab", tag="ds_then_w1", align_bytes=64)
+        nc.vector.memset(xs_tab[:].bitcast(I32), 0)
+        nc.vector.memset(ds_tab[:].bitcast(I32), 0)
+        nc.scalar.dma_start(xs_tab[0:P:8, :].bitcast(I32), x_scales[0].bitcast(I32))
+        nc.scalar.dma_start(ds_tab[0:P:8, :].bitcast(I32), d_scales[0].bitcast(I32))
+        dw_tab = keep.tile([P, T], I32, name="dw_tab", align_bytes=64)
+        xw_tab = keep.tile([P, T], I32, name="xw_tab", align_bytes=64)
+        nc.sync.dma_start(dw_tab[:], d_words[0].rearrange("p n r -> p (n r)").bitcast(I32))
+        n1_t = load_list("n1_t", n1)
+        n2_t = load_list("n2_t", n2)
+        n3_t = load_list("n3_t", n3)
+        n4_t = load_list("n4_t", n4)
+        nc.sync.dma_start(xw_tab[:], x_words[0].rearrange("p n r -> p (n r)").bitcast(I32))
+
+        x_plane = keep.tile([P, S], U8, name="x_plane", align_bytes=64)
+        d_plane = keep.tile([P, S], U8, name="d_plane", align_bytes=64)
+        w_plane_raw = keep.tile([P, S], U8, name="w_plane_raw", align_bytes=64)
+        nc.vector.memset(w_plane_raw[:].bitcast(I32), 0)
+        nc.vector.memset(x_plane[:].bitcast(I32), 0)
+        nc.vector.memset(d_plane[:].bitcast(I32), 0)
+        gn_t = keep.tile([P, PACK], F32, name="gn_t")
+        nc.gpsimd.dma_start(gn_t[:], gn.rearrange("(p t) o -> p (t o)", t=PACK))
+        for q in range(4):
+            nc.gpsimd.dma_start(
+                w_plane_raw[32 * q : 32 * q + 4, :].bitcast(I32), w1_scales[0, 4 * q : 4 * q + 4, :].bitcast(I32)
+            )
+
+        def place_scale_rows(plane, picked):
+            for q in range(4):
+                nc.scalar.dma_start(
+                    plane[32 * q : 32 * q + 4, :].bitcast(I32), picked[32 * q : 32 * q + 32 : 8, :].bitcast(I32)
+                )
+
+        halves = [slice(0, W), slice(W, S)]
+
+        def entries(cols):
+            return slice(cols.start // 16, cols.stop // 16)
+
+        xs_g = keep.tile([P, S], U8, name="xs_g", align_bytes=64)
+        nc.vector.tensor_copy(xs_g[:], xs_tab[:].indirect(offs_t[:]))
+        place_scale_rows(x_plane, xs_g)
+        ds_g = keep.tile([P, S], U8, name="ds_g", align_bytes=64)
+        nc.vector.tensor_copy(ds_g[:].rearrange("p (t m) -> p m t", t=PACK), ds_tab[:].indirect(ci_t[:]))
+        place_scale_rows(d_plane, ds_g)
+        dw_g = keep.tile([P, S], I32, name="dw_g", align_bytes=64)
+        nc.vector.tensor_copy(
+            dw_g[:].bitcast(U32).rearrange("p (t m) -> p m t", t=PACK), dw_tab[:].bitcast(U32).indirect(ci_t[:])
+        )
+        xw_g = keep.tile([P, S], I32, name="xw_g", align_bytes=64)
+        for c in halves:
+            nc.vector.tensor_copy(xw_g[:, c].bitcast(U32), xw_tab[:].bitcast(U32).indirect(offs_t[:, entries(c)]))
+
+        w_raw = keep.tile([P, 2 * S], U8, name="w_raw", tag="ds_then_w1", align_bytes=64)
+        nc.sync.dma_start(w_raw[:].bitcast(I32), w1_words[0].bitcast(I32))
+        w_codes = keep.tile([P, 2 * S], U8, name="w_codes", align_bytes=64)
+        w_plane = keep.tile([P, S], U8, name="w_plane", align_bytes=64)
+
+        def product(bank, cols, lhsT, lhsT_scale, rhs, rhs_scale):
+            acc = psum.tile([P, cols.stop - cols.start], F32, name="acc", tag=f"bank{bank}")
+            nc.tensor.matmul_mx(
+                out=acc[:],
+                lhsT=lhsT,
+                lhsT_scale=lhsT_scale,
+                rhs=rhs[:, cols].bitcast(FP8X4),
+                rhs_scale=rhs_scale[:, cols],
+                start=True,
+                stop=True,
+            )
+            return acc
+
+        zbs = [keep.tile([P, W, PACK], BF16, name=f"zb{i}", align_bytes=64) for i in range(2)]
+        dts = []
+        bank = 0
+        for t in range(PACK):
+            cols = slice(t * P, (t + 1) * P)
+            s_sb = keep.tile([P, S], F32, name=f"s_sb{t}")
+            for c in halves if t == 0 else [slice(0, S)]:
+                s_ps = product(bank, c, dw_g[:, cols].bitcast(FP8X4), d_plane[:, cols], xw_g, x_plane)
+                bank += 1
+                nc.scalar.activation(s_sb[:, c], s_ps[:], ACT.Copy, scale=0.0625)
+            pa = keep.tile([P, W], F32, name=f"pa{t}")
+            pb = keep.tile([P, W], F32, name=f"pb{t}")
+            nc.scalar.activation(pb[:], s_sb[:].indirect(n2_t[:]), ACT.Copy)
+            if t == 0:
+                nc.vector.tensor_copy(pa[:], s_sb[:].indirect(n1_t[:]))
+            else:
+                nc.scalar.activation(pa[:], s_sb[:].indirect(n1_t[:]), ACT.Copy)
+            mag = keep.tile([P, W], F32, name=f"mag{t}")
+            root = keep.tile([P, W], F32, name=f"root{t}")
+            inv = keep.tile([P, W], F32, name=f"inv{t}")
+            nc.scalar.activation(mag[:], pb[:], ACT.Abs)
+            nc.scalar.activation(root[:], mag[:], ACT.Abs_reciprocal_sqrt, bias=0.5)
+            nc.scalar.activation(inv[:], root[:], ACT.Square)
+            rb = keep.tile([P, W], F32, name=f"rb{t}")
+            nc.vector.tensor_tensor(rb[:], pa[:], pb[:], ALU.max)
+            dt = keep.tile([P, S], F32, name=f"dt{t}")
+            nc.vector.tensor_copy(dt[:].indirect(n2_t[:]), rb[:])
+            nc.vector.tensor_tensor(dt[:].indirect(n1_t[:]), pa[:], inv[:], ALU.mult)
+            dts.append(dt)
+        nc.vector.tensor_copy(
+            w_plane[:].rearrange("p (t m) -> p t m", t=PACK),
+            w_plane_raw[:].rearrange("p (m t) -> p t m", t=PACK),
+        )
+        for t in range(PACK):
+            for zb, c in zip(zbs, halves):
+                if t < 2:
+                    nc.scalar.activation(zb[:, :, t], dts[t][:, c], ACT.Copy, scale=gn_t[:, t : t + 1])
+                else:
+                    nc.vector.tensor_scalar(zb[:, :, t], dts[t][:, c], gn_t[:, t : t + 1], None, ALU.mult)
+        nc.scalar.copy(
+            w_codes[:].bitcast(U16).rearrange("p (t m) -> p t m", t=PACK),
+            w_raw[:].bitcast(U16).rearrange("p (m t) -> p t m", t=PACK),
+        )
+
+        z_codes = keep.tile([P, S], U32, name="z_codes", align_bytes=64)
+        z_plane = keep.tile([P, S], U8, name="z_plane", align_bytes=64)
+        for zb, c in zip(zbs, halves):
+            nc.vector.quantize_mx(
+                out=z_codes[:, c].bitcast(FP8X4), scales=z_plane[:, c], in_=zb[:].rearrange("p j t -> p (j t)")
+            )
+
+        out_rows = out.rearrange("(p t) n -> t p n", t=PACK)
+        for t in range(PACK):
+            lhsT = w_codes[:, 2 * P * t : 2 * P * (t + 1)].bitcast(FP4X4)
+            lhsT_scale = w_plane[:, t * P : (t + 1) * P]
+            h_sb = keep.tile([P, S], F32, name=f"h_sb{t}")
+            hop = keep.tile([P, S], F32, name=f"hop{t}")
+            st = keep.tile([P, S], F32, name=f"st{t}")
+            res = keep.tile([P, S], F32, name=f"res{t}")
+            if t == 0:
+                sent = keep.tile([P, S], F32, name=f"sent{t}")
+                h_ps = []
+                for c in halves:
+                    acc = product(bank % 8, c, lhsT, lhsT_scale, z_codes, z_plane)
+                    bank += 1
+                    nc.scalar.copy(h_sb[:, c], acc[:])
+                    h_ps.append(acc)
+                for c, h_part in ((slice(0, P), h_ps[0][:, 0:P]), (slice(P, W), h_ps[0][:, P:W]), (halves[1], h_ps[1][:])):
+                    nc.scalar.activation(hop[:, c], h_sb[:].indirect(n3_t[:, entries(c)]), ACT.Copy)
+                    nc.vector.tensor_tensor(st[:, c], h_part, hop[:, c], ALU.max)
+                    nc.vector.tensor_copy(sent[:].indirect(n4_t[:, entries(c)]), st[:, c])
+            else:
+                sent = keep.tile([P, 2 * S], F32, name=f"sent{t}")
+                acc = product(bank % 8, slice(0, S), lhsT, lhsT_scale, z_codes, z_plane)
+                bank += 1
+                nc.scalar.copy(h_sb[:], acc[:])
+                for c in halves:
+                    nc.scalar.activation(hop[:, c], h_sb[:].indirect(n3_t[:, entries(c)]), ACT.Copy)
+                nc.vector.tensor_tensor(st[:], acc[:], hop[:], ALU.max)
+                nc.vector.tensor_copy(sent[:].indirect(n4_t[:]), st[:])
+            if t < PACK - 1:
+                nc.gpsimd.tensor_tensor(res[:], sent[:, 0:S], h_sb[:], ALU.subtract)
+                nc.sync.dma_start(out_rows[t], res[:])
+            else:
+                for c, queue in zip(halves, (nc.sync, nc.scalar)):
+                    nc.vector.tensor_tensor(res[:, c], sent[:, c], acc[:, c], ALU.subtract)
+                    queue.dma_start(out_rows[t][:, c], res[:, c])

@@ -43,8 +43,12 @@ def tile_picked_hwlratiosendhop_none_p_kernel(
         nc.vector.memset(ds_tab[:].bitcast(I32), 0)
         nc.scalar.dma_start(xs_tab[0:P:8, :].bitcast(I32), x_scales[0].bitcast(I32))
         nc.scalar.dma_start(ds_tab[0:P:8, :].bitcast(I32), d_scales[0].bitcast(I32))
+        warm_in = keep.tile([P, 1], F32, name="warm_in")
+        warm_out = keep.tile([P, 1], F32, name="warm_out")
+        nc.vector.memset(warm_in[:], 1.0)
+        nc.scalar.activation(warm_out[:], warm_in[:], ACT.Abs_reciprocal_sqrt, bias=0.5)
         dw_tab = keep.tile([P, T], I32, name="dw_tab", align_bytes=64)
-        xw_tab = keep.tile([P, T], I32, name="xw_tab", align_bytes=64)
+        xw_tab = keep.tile([P, T], I32, name="xw_tab", tag="xw_then_w_plane", align_bytes=64)
         nc.sync.dma_start(dw_tab[:], d_words[0].rearrange("p n r -> p (n r)").bitcast(I32))
         n1_t = load_list("n1_t", n1)
         n2_t = load_list("n2_t", n2)
@@ -67,7 +71,7 @@ def tile_picked_hwlratiosendhop_none_p_kernel(
 
         def place_scale_rows(plane, picked):
             for q in range(4):
-                nc.scalar.dma_start(
+                nc.sync.dma_start(
                     plane[32 * q : 32 * q + 4, :].bitcast(I32), picked[32 * q : 32 * q + 32 : 8, :].bitcast(I32)
                 )
 
@@ -92,8 +96,11 @@ def tile_picked_hwlratiosendhop_none_p_kernel(
 
         w_raw = keep.tile([P, 2 * S], U8, name="w_raw", tag="ds_then_w1", align_bytes=64)
         nc.sync.dma_start(w_raw[:].bitcast(I32), w1_words[0].bitcast(I32))
-        w_codes = keep.tile([P, 2 * S], U8, name="w_codes", align_bytes=64)
-        w_plane = keep.tile([P, S], U8, name="w_plane", align_bytes=64)
+        w_plane = keep.tile([P, S], U8, name="w_plane", tag="xw_then_w_plane", align_bytes=64)
+        nc.vector.tensor_copy(
+            w_plane[:].rearrange("p (t m) -> p t m", t=PACK),
+            w_plane_raw[:].rearrange("p (m t) -> p t m", t=PACK),
+        )
 
         def product(bank, cols, lhsT, lhsT_scale, rhs, rhs_scale):
             acc = psum.tile([P, cols.stop - cols.start], F32, name="acc", tag=f"bank{bank}")
@@ -109,44 +116,57 @@ def tile_picked_hwlratiosendhop_none_p_kernel(
             return acc
 
         zbs = [keep.tile([P, W, PACK], BF16, name=f"zb{i}", align_bytes=64) for i in range(2)]
-        dts = []
+        s_tags = ["s0", "s0", "mag0", "mag1"]
+        inv_tags = ["inv0", "mag0", "mag1", "inv3"]
+        dt_tags = ["dt0", "dt1", "root1", "root2"]
+        dts, pas, rbs, roots = [], [], [], []
+
+        def send_larger(t):
+            dt = keep.tile([P, S], F32, name="dt", tag=dt_tags[t], align_bytes=64)
+            nc.vector.tensor_copy(dt[:].indirect(n2_t[:]), rbs[t][:])
+            dts.append(dt)
+
+        def send_ratio(t):
+            inv = keep.tile([P, W], F32, name="inv", tag=inv_tags[t])
+            nc.scalar.activation(inv[:], roots[t][:], ACT.Square)
+            nc.vector.tensor_tensor(dts[t][:].indirect(n1_t[:]), pas[t][:], inv[:], ALU.mult)
+
         bank = 0
         for t in range(PACK):
             cols = slice(t * P, (t + 1) * P)
-            s_sb = keep.tile([P, S], F32, name=f"s_sb{t}")
+            s_sb = keep.tile([P, S], F32, name="s_sb", tag=s_tags[t])
             for c in halves if t == 0 else [slice(0, S)]:
                 s_ps = product(bank, c, dw_g[:, cols].bitcast(FP8X4), d_plane[:, cols], xw_g, x_plane)
                 bank += 1
                 nc.scalar.activation(s_sb[:, c], s_ps[:], ACT.Copy, scale=0.0625)
-            pa = keep.tile([P, W], F32, name=f"pa{t}")
+            pa = keep.tile([P, W], F32, name="pa", tag="root0" if t == 1 else f"pa{t}", align_bytes=64)
             pb = keep.tile([P, W], F32, name=f"pb{t}")
+            rb = keep.tile([P, W], F32, name=f"rb{t}")
             nc.scalar.activation(pb[:], s_sb[:].indirect(n2_t[:]), ACT.Copy)
             if t == 0:
                 nc.vector.tensor_copy(pa[:], s_sb[:].indirect(n1_t[:]))
             else:
                 nc.scalar.activation(pa[:], s_sb[:].indirect(n1_t[:]), ACT.Copy)
-            mag = keep.tile([P, W], F32, name=f"mag{t}")
-            root = keep.tile([P, W], F32, name=f"root{t}")
-            inv = keep.tile([P, W], F32, name=f"inv{t}")
+            nc.vector.tensor_tensor(rb[:], pa[:], pb[:], ALU.max)
+            pas.append(pa)
+            rbs.append(rb)
+            if t >= 2:
+                send_ratio(t - 1)
+            send_larger(t)
+            mag = keep.tile([P, W], F32, name="mag", tag=f"mag{t}")
+            root = keep.tile([P, W], F32, name="root", tag=f"root{t}", align_bytes=64)
             nc.scalar.activation(mag[:], pb[:], ACT.Abs)
             nc.scalar.activation(root[:], mag[:], ACT.Abs_reciprocal_sqrt, bias=0.5)
-            nc.scalar.activation(inv[:], root[:], ACT.Square)
-            rb = keep.tile([P, W], F32, name=f"rb{t}")
-            nc.vector.tensor_tensor(rb[:], pa[:], pb[:], ALU.max)
-            dt = keep.tile([P, S], F32, name=f"dt{t}")
-            nc.vector.tensor_copy(dt[:].indirect(n2_t[:]), rb[:])
-            nc.vector.tensor_tensor(dt[:].indirect(n1_t[:]), pa[:], inv[:], ALU.mult)
-            dts.append(dt)
-        nc.vector.tensor_copy(
-            w_plane[:].rearrange("p (t m) -> p t m", t=PACK),
-            w_plane_raw[:].rearrange("p (m t) -> p t m", t=PACK),
-        )
+            roots.append(root)
+            if t in (0, PACK - 1):
+                send_ratio(t)
         for t in range(PACK):
             for zb, c in zip(zbs, halves):
-                if t < 2:
+                if t < 2 or c.start > 0:
                     nc.scalar.activation(zb[:, :, t], dts[t][:, c], ACT.Copy, scale=gn_t[:, t : t + 1])
                 else:
                     nc.vector.tensor_scalar(zb[:, :, t], dts[t][:, c], gn_t[:, t : t + 1], None, ALU.mult)
+        w_codes = keep.tile([P, 2 * S], U8, name="w_codes", tag="root3", align_bytes=64)
         nc.scalar.copy(
             w_codes[:].bitcast(U16).rearrange("p (t m) -> p t m", t=PACK),
             w_raw[:].bitcast(U16).rearrange("p (m t) -> p t m", t=PACK),
@@ -160,38 +180,55 @@ def tile_picked_hwlratiosendhop_none_p_kernel(
             )
 
         out_rows = out.rearrange("(p t) n -> t p n", t=PACK)
+        h_sbs, sts, accs = [], [], []
+
+        def send(t, sent):
+            res = keep.tile([P, S], F32, name=f"res{t}")
+            if t > 0:
+                nc.vector.tensor_copy(sent[:].indirect(n4_t[:]), sts[t][:])
+            if t < PACK - 1:
+                nc.gpsimd.tensor_tensor(res[:], sent[:, 0:S], h_sbs[t][:], ALU.subtract)
+                nc.sync.dma_start(out_rows[t], res[:])
+            else:
+                for c, queue in zip(halves, (nc.sync, nc.scalar)):
+                    nc.vector.tensor_tensor(res[:, c], sent[:, c], accs[t][:, c], ALU.subtract)
+                    queue.dma_start(out_rows[t][:, c], res[:, c])
+
         for t in range(PACK):
             lhsT = w_codes[:, 2 * P * t : 2 * P * (t + 1)].bitcast(FP4X4)
             lhsT_scale = w_plane[:, t * P : (t + 1) * P]
-            h_sb = keep.tile([P, S], F32, name=f"h_sb{t}")
-            hop = keep.tile([P, S], F32, name=f"hop{t}")
+            h_sb = keep.tile([P, S], F32, name="h_sb", tag="hop0_0" if t == 1 else f"h_sb{t}")
             st = keep.tile([P, S], F32, name=f"st{t}")
-            res = keep.tile([P, S], F32, name=f"res{t}")
+            h_sbs.append(h_sb)
+            sts.append(st)
             if t == 0:
-                sent = keep.tile([P, S], F32, name=f"sent{t}")
-                h_ps = []
+                sent = keep.tile([P, 2 * S], F32, name="sent0")
                 for c in halves:
                     acc = product(bank % 8, c, lhsT, lhsT_scale, z_codes, z_plane)
                     bank += 1
                     nc.scalar.copy(h_sb[:, c], acc[:])
-                    h_ps.append(acc)
-                for c, h_part in ((slice(0, P), h_ps[0][:, 0:P]), (slice(P, W), h_ps[0][:, P:W]), (halves[1], h_ps[1][:])):
-                    nc.scalar.activation(hop[:, c], h_sb[:].indirect(n3_t[:, entries(c)]), ACT.Copy)
-                    nc.vector.tensor_tensor(st[:, c], h_part, hop[:, c], ALU.max)
+                accs.append(None)
+                for c, pieces in ((slice(0, P), [slice(0, P)]), (slice(P, S), [slice(P, W), slice(W, S)])):
+                    hop = keep.tile([P, c.stop - c.start], F32, name="hop", tag=f"hop0_{c.start}")
+                    for piece in pieces:
+                        nc.scalar.activation(
+                            hop[:, piece.start - c.start : piece.stop - c.start],
+                            h_sb[:].indirect(n3_t[:, entries(piece)]),
+                            ACT.Copy,
+                        )
+                    nc.vector.tensor_tensor(st[:, c], h_sb[:, c], hop[:], ALU.max)
                     nc.vector.tensor_copy(sent[:].indirect(n4_t[:, entries(c)]), st[:, c])
+                send(t, sent)
             else:
-                sent = keep.tile([P, 2 * S], F32, name=f"sent{t}")
                 acc = product(bank % 8, slice(0, S), lhsT, lhsT_scale, z_codes, z_plane)
+                accs.append(acc)
                 bank += 1
                 nc.scalar.copy(h_sb[:], acc[:])
-                for c in halves:
-                    nc.scalar.activation(hop[:, c], h_sb[:].indirect(n3_t[:, entries(c)]), ACT.Copy)
-                nc.vector.tensor_tensor(st[:], acc[:], hop[:], ALU.max)
-                nc.vector.tensor_copy(sent[:].indirect(n4_t[:]), st[:])
-            if t < PACK - 1:
-                nc.gpsimd.tensor_tensor(res[:], sent[:, 0:S], h_sb[:], ALU.subtract)
-                nc.sync.dma_start(out_rows[t], res[:])
-            else:
-                for c, queue in zip(halves, (nc.sync, nc.scalar)):
-                    nc.vector.tensor_tensor(res[:, c], sent[:, c], acc[:, c], ALU.subtract)
-                    queue.dma_start(out_rows[t][:, c], res[:, c])
+                for i, c in enumerate(halves):
+                    hop = keep.tile([P, W], F32, name="hop", tag=f"hop{t}_{i}")
+                    nc.scalar.activation(hop[:], h_sb[:].indirect(n3_t[:, entries(c)]), ACT.Copy)
+                    nc.vector.tensor_tensor(st[:, c], acc[:, c], hop[:], ALU.max)
+                    if t == 2 and i == 0:
+                        send(1, keep.tile([P, 2 * S], F32, name="sent1", tag="hop2_0"))
+        send(2, keep.tile([P, 2 * S], F32, name="sent2", tag="hop3_0"))
+        send(3, keep.tile([P, 2 * S], F32, name="sent3"))

@@ -38,7 +38,7 @@ def tile_picked_hwlratiosendhop_none_p_kernel(
         offs_t = load_list("offs_t", offs)
         ci_t = load_list("ci_t", ci)
         xs_tab = keep.tile([P, T], U8, name="xs_tab", align_bytes=64)
-        ds_tab = keep.tile([P, T], U8, name="ds_tab", tag="ds_then_w1", align_bytes=64)
+        ds_tab = keep.tile([P, T], U8, name="ds_tab", align_bytes=64)
         nc.vector.memset(xs_tab[:].bitcast(I32), 0)
         nc.vector.memset(ds_tab[:].bitcast(I32), 0)
         nc.scalar.dma_start(xs_tab[0:P:8, :].bitcast(I32), x_scales[0].bitcast(I32))
@@ -69,6 +69,9 @@ def tile_picked_hwlratiosendhop_none_p_kernel(
                 w_plane_raw[32 * q : 32 * q + 4, :].bitcast(I32), w1_scales[0, 4 * q : 4 * q + 4, :].bitcast(I32)
             )
 
+        w_raw = keep.tile([P, 2 * S], U8, name="w_raw", align_bytes=64)
+        nc.gpsimd.dma_start(w_raw[:].bitcast(I32), w1_words[0].bitcast(I32))
+
         def place_scale_rows(plane, picked):
             for q in range(4):
                 nc.sync.dma_start(
@@ -94,8 +97,11 @@ def tile_picked_hwlratiosendhop_none_p_kernel(
         for c in halves:
             nc.vector.tensor_copy(xw_g[:, c].bitcast(U32), xw_tab[:].bitcast(U32).indirect(offs_t[:, entries(c)]))
 
-        w_raw = keep.tile([P, 2 * S], U8, name="w_raw", tag="ds_then_w1", align_bytes=64)
-        nc.sync.dma_start(w_raw[:].bitcast(I32), w1_words[0].bitcast(I32))
+        w_codes = keep.tile([P, 2 * S], U8, name="w_codes", align_bytes=64)
+        nc.scalar.copy(
+            w_codes[:].bitcast(U16).rearrange("p (t m) -> p t m", t=PACK),
+            w_raw[:].bitcast(U16).rearrange("p (m t) -> p t m", t=PACK),
+        )
         w_plane = keep.tile([P, S], U8, name="w_plane", tag="xw_then_w_plane", align_bytes=64)
         nc.vector.tensor_copy(
             w_plane[:].rearrange("p (t m) -> p t m", t=PACK),
@@ -166,11 +172,6 @@ def tile_picked_hwlratiosendhop_none_p_kernel(
                     nc.scalar.activation(zb[:, :, t], dts[t][:, c], ACT.Copy, scale=gn_t[:, t : t + 1])
                 else:
                     nc.vector.tensor_scalar(zb[:, :, t], dts[t][:, c], gn_t[:, t : t + 1], None, ALU.mult)
-        w_codes = keep.tile([P, 2 * S], U8, name="w_codes", tag="root3", align_bytes=64)
-        nc.scalar.copy(
-            w_codes[:].bitcast(U16).rearrange("p (t m) -> p t m", t=PACK),
-            w_raw[:].bitcast(U16).rearrange("p (m t) -> p t m", t=PACK),
-        )
 
         z_codes = keep.tile([P, S], U32, name="z_codes", align_bytes=64)
         z_plane = keep.tile([P, S], U8, name="z_plane", align_bytes=64)
@@ -197,16 +198,19 @@ def tile_picked_hwlratiosendhop_none_p_kernel(
         for t in range(PACK):
             lhsT = w_codes[:, 2 * P * t : 2 * P * (t + 1)].bitcast(FP4X4)
             lhsT_scale = w_plane[:, t * P : (t + 1) * P]
-            h_sb = keep.tile([P, S], F32, name="h_sb", tag="hop0_0" if t == 1 else f"h_sb{t}")
+            h_sb = keep.tile([P, S], F32, name="h_sb", tag=["h_sb0", "hop0_0", "hop0_128", "hop1_0"][t])
             st = keep.tile([P, S], F32, name=f"st{t}")
             h_sbs.append(h_sb)
             sts.append(st)
             if t == 0:
                 sent = keep.tile([P, 2 * S], F32, name="sent0")
-                for c in halves:
+                for c in (slice(0, W), slice(W, W + P), slice(W + P, S)):
                     acc = product(bank % 8, c, lhsT, lhsT_scale, z_codes, z_plane)
                     bank += 1
-                    nc.scalar.copy(h_sb[:, c], acc[:])
+                    if c.stop < S:
+                        nc.scalar.copy(h_sb[:, c], acc[:])
+                    else:
+                        nc.vector.tensor_copy(h_sb[:, c], acc[:])
                 accs.append(None)
                 for c, pieces in ((slice(0, P), [slice(0, P)]), (slice(P, S), [slice(P, W), slice(W, S)])):
                     hop = keep.tile([P, c.stop - c.start], F32, name="hop", tag=f"hop0_{c.start}")

from contextlib import ExitStack

import concourse.mybir as mybir

F32 = mybir.dt.float32
BF16 = mybir.dt.bfloat16
I32 = mybir.dt.int32
U32 = mybir.dt.uint32
U16 = mybir.dt.uint16
U8 = mybir.dt.uint8
FP8X4 = mybir.dt.float8_e4m3fn_x4
FP4X4 = mybir.dt.float4_e2m1fn_x4
ALU = mybir.AluOpType
ACT = mybir.ActivationFunctionType

P = 128
PACK = 4
T = 2048
S = 512
W = 256

FLOPS = 2 * 2 * 512 * 512 * 512


def tile_picked_hwlratiosendhop_none_p_kernel(
    tc, x_words, x_scales, d_words, d_scales, gn, w1_words, w1_scales, offs, ci, n1, n2, n3, n4, out
):
    nc = tc.nc
    with ExitStack() as ctx:
        keep = ctx.enter_context(tc.tile_pool(name="keep", bufs=1))
        psum = ctx.enter_context(tc.psum_pool(name="psum", bufs=1))

        def load_list(name, src):
            t = keep.tile(list(src.shape), U16, name=name)
            nc.sync.dma_start(t[:], src)
            return t

        offs_t = load_list("offs_t", offs)
        ci_t = load_list("ci_t", ci)
        xs_tab = keep.tile([P, T], U8, name="xs_tab", align_bytes=64)
        ds_tab = keep.tile([P, T], U8, name="ds_tab", align_bytes=64)
        nc.vector.memset(xs_tab[:].bitcast(I32), 0)
        nc.vector.memset(ds_tab[:].bitcast(I32), 0)
        nc.scalar.dma_start(xs_tab[0:P:8, :].bitcast(I32), x_scales[0].bitcast(I32))
        nc.scalar.dma_start(ds_tab[0:P:8, :].bitcast(I32), d_scales[0].bitcast(I32))
        warm_in = keep.tile([P, 1], F32, name="warm_in")
        warm_out = keep.tile([P, 1], F32, name="warm_out")
        nc.vector.memset(warm_in[:], 1.0)
        nc.scalar.activation(warm_out[:], warm_in[:], ACT.Abs_reciprocal_sqrt, bias=0.5)
        dw_tab = keep.tile([P, T], I32, name="dw_tab", align_bytes=64)
        xw_tab = keep.tile([P, T], I32, name="xw_tab", tag="xw_then_w_plane", align_bytes=64)
        nc.sync.dma_start(dw_tab[:], d_words[0].rearrange("p n r -> p (n r)").bitcast(I32))
        n1_t = load_list("n1_t", n1)
        n2_t = load_list("n2_t", n2)
        n3_t = load_list("n3_t", n3)
        n4_t = load_list("n4_t", n4)
        nc.sync.dma_start(xw_tab[:], x_words[0].rearrange("p n r -> p (n r)").bitcast(I32))

        x_plane = keep.tile([P, S], U8, name="x_plane", align_bytes=64)
        d_plane = keep.tile([P, S], U8, name="d_plane", align_bytes=64)
        w_plane_raw = keep.tile([P, S], U8, name="w_plane_raw", align_bytes=64)
        nc.vector.memset(w_plane_raw[:].bitcast(I32), 0)
        nc.vector.memset(x_plane[:].bitcast(I32), 0)
        nc.vector.memset(d_plane[:].bitcast(I32), 0)
        gn_t = keep.tile([P, PACK], F32, name="gn_t")
        nc.gpsimd.dma_start(gn_t[:], gn.rearrange("(p t) o -> p (t o)", t=PACK))
        for q in range(4):
            nc.gpsimd.dma_start(
                w_plane_raw[32 * q : 32 * q + 4, :].bitcast(I32), w1_scales[0, 4 * q : 4 * q + 4, :].bitcast(I32)
            )

        w_raw = keep.tile([P, 2 * S], U8, name="w_raw", align_bytes=64)
        nc.gpsimd.dma_start(w_raw[:].bitcast(I32), w1_words[0].bitcast(I32))

        def place_scale_rows(plane, picked):
            for q in range(4):
                nc.sync.dma_start(
                    plane[32 * q : 32 * q + 4, :].bitcast(I32), picked[32 * q : 32 * q + 32 : 8, :].bitcast(I32)
                )

        halves = [slice(0, W), slice(W, S)]

        def entries(cols):
            return slice(cols.start // 16, cols.stop // 16)

        xs_g = keep.tile([P, S], U8, name="xs_g", align_bytes=64)
        nc.vector.tensor_copy(xs_g[:], xs_tab[:].indirect(offs_t[:]))
        place_scale_rows(x_plane, xs_g)
        ds_g = keep.tile([P, S], U8, name="ds_g", align_bytes=64)
        nc.vector.tensor_copy(ds_g[:].rearrange("p (t m) -> p m t", t=PACK), ds_tab[:].indirect(ci_t[:]))
        place_scale_rows(d_plane, ds_g)
        dw_g = keep.tile([P, S], I32, name="dw_g", align_bytes=64)
        nc.vector.tensor_copy(
            dw_g[:].bitcast(U32).rearrange("p (t m) -> p m t", t=PACK), dw_tab[:].bitcast(U32).indirect(ci_t[:])
        )
        xw_g = keep.tile([P, S], I32, name="xw_g", align_bytes=64)
        for c in halves:
            nc.vector.tensor_copy(xw_g[:, c].bitcast(U32), xw_tab[:].bitcast(U32).indirect(offs_t[:, entries(c)]))

        w_codes = keep.tile([P, 2 * S], U8, name="w_codes", align_bytes=64)
        nc.scalar.copy(
            w_codes[:].bitcast(U16).rearrange("p (t m) -> p t m", t=PACK),
            w_raw[:].bitcast(U16).rearrange("p (m t) -> p t m", t=PACK),
        )
        w_plane = keep.tile([P, S], U8, name="w_plane", tag="xw_then_w_plane", align_bytes=64)
        nc.vector.tensor_copy(
            w_plane[:].rearrange("p (t m) -> p t m", t=PACK),
            w_plane_raw[:].rearrange("p (m t) -> p t m", t=PACK),
        )

        def product(bank, cols, lhsT, lhsT_scale, rhs, rhs_scale):
            acc = psum.tile([P, cols.stop - cols.start], F32, name="acc", tag=f"bank{bank}")
            nc.tensor.matmul_mx(
                out=acc[:],
                lhsT=lhsT,
                lhsT_scale=lhsT_scale,
                rhs=rhs[:, cols].bitcast(FP8X4),
                rhs_scale=rhs_scale[:, cols],
                start=True,
                stop=True,
            )
            return acc

        zbs = [keep.tile([P, W, PACK], BF16, name=f"zb{i}", align_bytes=64) for i in range(2)]
        s_tags = ["s0", "s0", "mag0", "mag1"]
        inv_tags = ["inv0", "mag0", "mag1", "inv3"]
        dt_tags = ["dt0", "dt1", "root1", "root2"]
        dts, pas, rbs, roots = [], [], [], []

        def send_larger(t):
            dt = keep.tile([P, S], F32, name="dt", tag=dt_tags[t], align_bytes=64)
            nc.vector.tensor_copy(dt[:].indirect(n2_t[:]), rbs[t][:])
            dts.append(dt)

        def send_ratio(t):
            inv = keep.tile([P, W], F32, name="inv", tag=inv_tags[t])
            nc.scalar.activation(inv[:], roots[t][:], ACT.Square)
            nc.vector.tensor_tensor(dts[t][:].indirect(n1_t[:]), pas[t][:], inv[:], ALU.mult)

        bank = 0
        for t in range(PACK):
            cols = slice(t * P, (t + 1) * P)
            s_sb = keep.tile([P, S], F32, name="s_sb", tag=s_tags[t])
            for c in halves if t == 0 else [slice(0, S)]:
                s_ps = product(bank, c, dw_g[:, cols].bitcast(FP8X4), d_plane[:, cols], xw_g, x_plane)
                bank += 1
                nc.scalar.activation(s_sb[:, c], s_ps[:], ACT.Copy, scale=0.0625)
            pa = keep.tile([P, W], F32, name="pa", tag="root0" if t == 1 else f"pa{t}", align_bytes=64)
            pb = keep.tile([P, W], F32, name=f"pb{t}")
            rb = keep.tile([P, W], F32, name=f"rb{t}")
            nc.scalar.activation(pb[:], s_sb[:].indirect(n2_t[:]), ACT.Copy)
            if t == 0:
                nc.vector.tensor_copy(pa[:], s_sb[:].indirect(n1_t[:]))
            else:
                nc.scalar.activation(pa[:], s_sb[:].indirect(n1_t[:]), ACT.Copy)
            nc.vector.tensor_tensor(rb[:], pa[:], pb[:], ALU.max)
            pas.append(pa)
            rbs.append(rb)
            if t >= 2:
                send_ratio(t - 1)
            send_larger(t)
            mag = keep.tile([P, W], F32, name="mag", tag=f"mag{t}")
            root = keep.tile([P, W], F32, name="root", tag=f"root{t}", align_bytes=64)
            nc.scalar.activation(mag[:], pb[:], ACT.Abs)
            nc.scalar.activation(root[:], mag[:], ACT.Abs_reciprocal_sqrt, bias=0.5)
            roots.append(root)
            if t in (0, PACK - 1):
                send_ratio(t)
        for t in range(PACK):
            for zb, c in zip(zbs, halves):
                if t < 2 or c.start > 0:
                    nc.scalar.activation(zb[:, :, t], dts[t][:, c], ACT.Copy, scale=gn_t[:, t : t + 1])
                else:
                    nc.vector.tensor_scalar(zb[:, :, t], dts[t][:, c], gn_t[:, t : t + 1], None, ALU.mult)

        z_codes = keep.tile([P, S], U32, name="z_codes", align_bytes=64)
        z_plane = keep.tile([P, S], U8, name="z_plane", align_bytes=64)
        for zb, c in zip(zbs, halves):
            nc.vector.quantize_mx(
                out=z_codes[:, c].bitcast(FP8X4), scales=z_plane[:, c], in_=zb[:].rearrange("p j t -> p (j t)")
            )

        out_rows = out.rearrange("(p t) n -> t p n", t=PACK)
        h_sbs, sts, accs = [], [], []

        def send(t, sent):
            res = keep.tile([P, S], F32, name=f"res{t}")
            if t > 0:
                nc.vector.tensor_copy(sent[:].indirect(n4_t[:]), sts[t][:])
            if t < PACK - 1:
                nc.gpsimd.tensor_tensor(res[:], sent[:, 0:S], h_sbs[t][:], ALU.subtract)
                nc.sync.dma_start(out_rows[t], res[:])
            else:
                for c, queue in zip(halves, (nc.sync, nc.scalar)):
                    nc.vector.tensor_tensor(res[:, c], sent[:, c], accs[t][:, c], ALU.subtract)
                    queue.dma_start(out_rows[t][:, c], res[:, c])

        for t in range(PACK):
            lhsT = w_codes[:, 2 * P * t : 2 * P * (t + 1)].bitcast(FP4X4)
            lhsT_scale = w_plane[:, t * P : (t + 1) * P]
            h_sb = keep.tile([P, S], F32, name="h_sb", tag=["h_sb0", "hop0_0", "hop0_128", "hop1_0"][t])
            st = keep.tile([P, S], F32, name=f"st{t}")
            h_sbs.append(h_sb)
            sts.append(st)
            if t == 0:
                sent = keep.tile([P, 2 * S], F32, name="sent0")
                for c in (slice(0, W), slice(W, W + P), slice(W + P, S)):
                    acc = product(bank % 8, c, lhsT, lhsT_scale, z_codes, z_plane)
                    bank += 1
                    if c.stop < S:
                        nc.scalar.copy(h_sb[:, c], acc[:])
                    else:
                        nc.vector.tensor_copy(h_sb[:, c], acc[:])
                accs.append(None)
                for c, pieces in ((slice(0, P), [slice(0, P)]), (slice(P, S), [slice(P, W), slice(W, S)])):
                    hop = keep.tile([P, c.stop - c.start], F32, name="hop", tag=f"hop0_{c.start}")
                    for piece in pieces:
                        nc.scalar.activation(
                            hop[:, piece.start - c.start : piece.stop - c.start],
                            h_sb[:].indirect(n3_t[:, entries(piece)]),
                            ACT.Copy,
                        )
                    nc.vector.tensor_tensor(st[:, c], h_sb[:, c], hop[:], ALU.max)
                    nc.vector.tensor_copy(sent[:].indirect(n4_t[:, entries(c)]), st[:, c])
                send(t, sent)
            else:
                acc = product(bank % 8, slice(0, S), lhsT, lhsT_scale, z_codes, z_plane)
                accs.append(acc)
                bank += 1
                nc.scalar.copy(h_sb[:], acc[:])
                for i, c in enumerate(halves):
                    hop = keep.tile([P, W], F32, name="hop", tag=f"hop{t}_{i}")
                    nc.scalar.activation(hop[:], h_sb[:].indirect(n3_t[:, entries(c)]), ACT.Copy)
                    nc.vector.tensor_tensor(st[:, c], acc[:, c], hop[:], ALU.max)
                    if t == 2 and i == 0:
                        send(1, keep.tile([P, 2 * S], F32, name="sent1", tag="hop2_0"))
        send(2, keep.tile([P, 2 * S], F32, name="sent2", tag="hop3_0"))
        send(3, keep.tile([P, 2 * S], F32, name="sent3"))
